import numpy as np
import ml_dtypes


def mxq(x, axis, fmt="e4m3"):
    dtype, down = {"e4m3": (ml_dtypes.float8_e4m3fn, 7), "e5m2": (ml_dtypes.float8_e5m2, 14)}[fmt]
    v = np.moveaxis(np.asarray(x, np.float32).astype(ml_dtypes.bfloat16).astype(np.float64), axis, -1)
    blocks = v.reshape(v.shape[:-1] + (-1, 32))
    amax = np.abs(blocks).max(-1, keepdims=True)
    byte = np.maximum(np.where(amax > 0, np.frexp(amax)[1] - 1 + 127, 0) - down, 1)
    scale = np.exp2(byte - 127.0)
    codes = (blocks / scale).astype(np.float32).astype(dtype).astype(np.float64)
    return np.moveaxis((codes * scale).reshape(v.shape), -1, axis)


WIDE = False


def mx_kscale(k):
    if not WIDE:
        return np.ones(k)
    levels = np.array([10, -10, 5, -5, 0])
    if k % 512:
        return np.exp2(np.random.permutation(np.resize(levels, k // 32))).repeat(32)
    a = np.empty((k // 512, 16))
    for p in range(k // 512):
        a[p, :8] = np.random.permutation(np.resize(levels, 8))
        for g in range(8):
            far = levels[np.abs(levels - a[p, g]) >= 10]
            a[p, g + 8] = far[np.random.randint(len(far))]
    return np.exp2(a.ravel()).repeat(32)


BF16 = ml_dtypes.bfloat16


def bf(x):
    return np.asarray(x, np.float32).astype(BF16)


def f64(x):
    return np.asarray(x).astype(np.float64)


E2M1 = np.array([0.0, 0.5, 1.0, 1.5, 2.0, 3.0, 4.0, 6.0, -0.0, -0.5, -1.0, -1.5, -2.0, -3.0, -4.0, -6.0])


def pack_weight(w, fmt):
    k, n = w.shape
    w = f64(bf(w)).reshape(k // 32, 32, n)
    amax = np.abs(w).max(1)
    if fmt == "e4m3":
        byte = np.frexp(amax)[1] - 1 + 127 - 7
    else:
        mant, ex = np.frexp(amax / 6.0)
        byte = np.where(mant > 0.5, ex, ex - 1) + 127
    byte = np.clip(np.where(amax > 0, byte, 1), 1, 254)
    scaled = (w * np.exp2(127.0 - byte)[:, None, :]).reshape(k, n).astype(np.float32)
    by_word = np.ascontiguousarray(scaled.reshape(k // 512, 128, 4, n).transpose(0, 1, 3, 2))
    if fmt == "e4m3":
        words = by_word.astype(ml_dtypes.float8_e4m3fn).view(np.uint8)
    else:
        c = by_word.astype(ml_dtypes.float4_e2m1fn).view(np.uint8) & 0xF
        words = c[..., 0::2] | (c[..., 1::2] << 4)
    return np.ascontiguousarray(words), np.ascontiguousarray(byte.astype(np.uint8).reshape(k // 512, 16, n))


def unpack_weight(words, scales, fmt):
    g, p, n, _ = words.shape
    if fmt == "e4m3":
        vals = np.ascontiguousarray(words).view(ml_dtypes.float8_e4m3fn).astype(np.float64)
    else:
        nib = np.empty((g, p, n, 4), np.uint8)
        nib[..., 0::2] = words & 0xF
        nib[..., 1::2] = words >> 4
        vals = E2M1[nib]
    vals = vals * np.repeat(np.exp2(scales.astype(np.float64) - 127.0), 8, axis=1)[..., None]
    return vals.transpose(0, 1, 3, 2).reshape(g * 512, n)
def pack4(w):
    words, scales = pack_weight(w, "e2m1")
    return words.reshape(words.shape[0], 128, -1), scales


def unpack4(words, scales):
    return unpack_weight(words.reshape(words.shape[0], 128, -1, 2), scales, "e2m1")


B, S, D, R, Q = 4, 1024, 1024, 512, 512


def smoothed_signed_sqrt(p):
    return p / np.sqrt(np.abs(p) + 0.1)


def matrix_rms_normalize(y):
    mean_sq = np.mean(y * y, axis=(1, 2), keepdims=True)
    return y / np.sqrt(mean_sq + 1e-5)


def draw0():
    s, t = mx_kscale(S), mx_kscale(D)
    amp = 2.0 ** np.linspace(-1.0, 1.0, B)
    x = bf(np.random.standard_normal((B, S, D)) * amp[:, None, None] / s[None, :, None])
    u_words, u_scales = pack4(np.random.standard_normal((S, R)) / np.sqrt(S) * s[:, None])
    c = bf(np.random.standard_normal(R) * 0.5)
    g = bf((1.0 + 0.1 * np.random.standard_normal(D)) * t)
    v_words, v_scales = pack4(np.random.standard_normal((D, Q)) * 1.5 / np.sqrt(D) / t[:, None])
    return {"x": x,
            "u_words": u_words,
            "u_scales": u_scales,
            "c": c,
            "g": g,
            "v_words": v_words,
            "v_scales": v_scales}


def core(x, u_words, u_scales, c, g, v_words, v_scales):
    uq = unpack4(u_words, u_scales)
    xq = mxq(f64(x), 1, "e4m3")
    p = uq.T @ xq
    p = p + f64(c)[None, :, None]
    z = smoothed_signed_sqrt(p)
    z = z * f64(g)[None, None, :]
    y = mxq(z, 2, "e4m3") @ unpack4(v_words, v_scales)
    return matrix_rms_normalize(y)


def e4m3fn_bytes(y):
    return np.clip(np.asarray(y, np.float64), -448.0, 448.0).astype(np.float32).astype(ml_dtypes.float8_e4m3fn).view(np.uint8)


def e4m3fn_values(b):
    return np.asarray(b, np.uint8).view(ml_dtypes.float8_e4m3fn).astype(np.float64)


def setup_inputs():
    d = draw0()
    x0 = np.asarray(d['x']).astype(np.float64)
    s = (np.max(np.abs(x0), axis=(0, 2), keepdims=True) / 448.0).astype(np.float32)
    out = {}
    for k, v in d.items():
        if k == 'x':
            out['x_bytes'] = e4m3fn_bytes(x0 / s.astype(np.float64))
            out['x_scale'] = s
        else:
            out[k] = v
    return out


def reference(x_bytes, x_scale, u_words, u_scales, c, g, v_words, v_scales):
    return core(e4m3fn_values(x_bytes) * x_scale.astype(np.float64), u_words, u_scales, c, g, v_words, v_scales)

@@ -1,0 +1,317 @@
+from contextlib import ExitStack
+
+import concourse.mybir as mybir
+from concourse.masks import make_identity
+
+B, S, D, R, Q = 4, 1024, 1024, 512, 512
+FLOPS = B * (2 * S * R * D + 2 * R * D * Q)
+
+F32 = mybir.dt.float32
+BF16 = mybir.dt.bfloat16
+I32 = mybir.dt.int32
+U32 = mybir.dt.uint32
+U8 = mybir.dt.uint8
+FP8 = mybir.dt.float8_e4m3fn
+FP8X4 = mybir.dt.float8_e4m3fn_x4
+FP4X4 = mybir.dt.float4_e2m1fn_x4
+ACT = mybir.ActivationFunctionType
+ALU = mybir.AluOpType
+
+P = 128
+PACK = 4
+K_PASS = P * PACK
+BANK = 512
+PASSES = S // K_PASS
+HALVES = D // BANK
+ROW_TILES = R // P
+UNITS = B * ROW_TILES
+CHUNKS = B * HALVES * PASSES
+QUANT_LEAD = 5
+LAST_STEP = UNITS + 1
+
+
+def scalar_share(step):
+    if step == -QUANT_LEAD - 1:
+        return 1024
+    if step < -1:
+        return 1792
+    if step == -1:
+        return 512
+    if step == 0:
+        return 1024
+    if step < 5:
+        return 1536
+    return 1408
+
+
+def tile_tuckertwopowerpooling_w4_kernel(
+    tc, x_bytes, x_scale, u_words, u_scales, c, g, v_words, v_scales, out
+):
+    nc = tc.nc
+    with ExitStack() as ctx:
+        keep = ctx.enter_context(tc.tile_pool(name="keep", bufs=1))
+        work = ctx.enter_context(tc.tile_pool(name="work", bufs=2))
+        codes = ctx.enter_context(tc.tile_pool(name="codes", bufs=2 * HALVES * PASSES))
+        results = ctx.enter_context(tc.tile_pool(name="results", bufs=4))
+        psum = ctx.enter_context(tc.psum_pool(name="psum", bufs=1))
+        ctx.enter_context(tc.manual_schedule())
+        ctx.enter_context(nc.allow_non_contiguous_dma(reason="small vectors go one row to a partition"))
+
+        u_w = keep.tile([P, PASSES, 2 * R], U8, name="u_w", align_bytes=64)
+        u_s = keep.tile([P, PASSES, R], U8, name="u_s", align_bytes=64)
+        v_w = keep.tile([P, HALVES, 2 * Q], U8, name="v_w", align_bytes=64)
+        v_s = keep.tile([P, HALVES, Q], U8, name="v_s", align_bytes=64)
+        row_scale = keep.tile([P, PASSES, PACK], F32, name="row_scale")
+        c_bf = keep.tile([P, ROW_TILES, 2], BF16, name="c_bf")
+        g_bf = keep.tile([P, HALVES, PACK], BF16, name="g_bf")
+        bias = keep.tile([P, ROW_TILES], F32, name="bias")
+        gain = keep.tile([P, HALVES, PACK], F32, name="gain")
+        ident = keep.tile([P, P], F32, name="ident")
+        ones = keep.tile([P, P], F32, name="ones")
+
+        nc.vector.memset(u_s[:].rearrange("p g n -> p (g n)").bitcast(I32), 0)
+        nc.vector.memset(v_s[:].rearrange("p g n -> p (g n)").bitcast(I32), 0)
+        make_identity(nc, ident[:])
+        nc.gpsimd.memset(ones[:], 1.0)
+
+        xb = {}
+
+        def load_x(j):
+            b, h, k = j // 4, (j // 2) % 2, j % 2
+            xb[j] = keep.tile([P, PACK, BANK], U8, name="xb%d" % j)
+            rows = x_bytes[b, k * K_PASS : (k + 1) * K_PASS, h * BANK : (h + 1) * BANK]
+            nc.sync.dma_start(out=xb[j][:], in_=rows.rearrange("(p t) d -> p t d", t=PACK))
+
+        def load_weight(words_sb, scales_sb, words, scales):
+            nc.sync.dma_start(
+                out=words_sb[:].bitcast(I32), in_=words.rearrange("k p n -> p k n").bitcast(I32)
+            )
+            for q in range(4):
+                nc.sync.dma_start(
+                    out=scales_sb[32 * q : 32 * q + 4, :, :].bitcast(I32),
+                    in_=scales[:, 4 * q : 4 * q + 4, :].rearrange("k r n -> r k n").bitcast(I32),
+                )
+
+        load_x(0)
+        nc.sync.dma_start(
+            out=row_scale[:], in_=x_scale.rearrange("o (k p t) e -> p (o k) (t e)", p=P, t=PACK)
+        )
+        load_x(1)
+        load_x(2)
+        load_weight(u_w, u_s, u_words, u_scales)
+        load_x(3)
+        nc.sync.dma_start(out=c_bf[:, :, 0:1], in_=c.rearrange("(i p e) -> p i e", p=P, e=1))
+        nc.sync.dma_start(out=g_bf[:], in_=g.rearrange("(h p t) -> p h t", p=P, t=PACK))
+        load_x(4)
+        load_weight(v_w, v_s, v_words, v_scales)
+        for j in range(5, CHUNKS):
+            load_x(j)
+
+        wide, inter, xq, xs = {}, {}, {}, {}
+        acc, mag, inv, pre, turned, z_bf, zq, zs, y = {}, {}, {}, {}, {}, {}, {}, {}, {}
+        sums, total, norm = {}, {}, {}
+
+        def widen_pieces(j, on_scalar):
+            if not 0 <= j < CHUNKS:
+                return []
+            share = scalar_share(j - QUANT_LEAD - 1)
+            pieces = []
+            for t in range(PACK):
+                cut = min(max(share - t * BANK, 0), BANK)
+                lo, hi = (0, cut) if on_scalar else (cut, BANK)
+                if hi > lo:
+                    pieces.append((j, t, lo, hi))
+            return pieces
+
+        def widen(piece, on_scalar):
+            j, t, lo, hi = piece
+            if j not in wide:
+                wide[j] = work.tile([P, PACK, BANK], BF16, name="wide", bufs=3)
+            src = xb[j][:, t, lo:hi].bitcast(FP8)
+            factor = row_scale[:, j % 2, t : t + 1]
+            if on_scalar:
+                nc.scalar.activation(out=wide[j][:, t, lo:hi], in_=src, func=ACT.Copy, scale=factor)
+            else:
+                nc.vector.tensor_scalar(
+                    out=wide[j][:, t, lo:hi], in0=src, scalar1=factor, scalar2=None, op0=ALU.mult
+                )
+
+        def interleave(j):
+            inter[j] = work.tile([P, BANK, PACK], BF16, name="inter", align_bytes=64)
+            nc.vector.tensor_copy(
+                out=inter[j][:].rearrange("p (c i) t -> p c t i", i=4),
+                in_=wide[j][:].rearrange("p t (c i) -> p c t i", i=4),
+            )
+
+        def quantize_x(j):
+            xq[j] = codes.tile([P, BANK], U32, name="xq", align_bytes=64)
+            xs[j] = codes.tile([P, BANK], U8, name="xs", align_bytes=64)
+            nc.vector.quantize_mx(
+                out=xq[j][:].bitcast(FP8X4), scales=xs[j][:], in_=inter[j][:].rearrange("p d t -> p (d t)")
+            )
+
+        def first_product(n, h):
+            b, i = divmod(n, ROW_TILES)
+            acc[n, h] = psum.tile([P, BANK], F32, name="acc%d" % h)
+            for k in range(PASSES):
+                j = 4 * b + 2 * h + k
+                nc.tensor.matmul_mx(
+                    out=acc[n, h][:],
+                    lhsT=u_w[:, k, 2 * P * i : 2 * P * (i + 1)].bitcast(FP4X4),
+                    lhsT_scale=u_s[:, k, P * i : P * (i + 1)],
+                    rhs=xq[j][:].bitcast(FP8X4),
+                    rhs_scale=xs[j][:],
+                    start=(k == 0),
+                    stop=(k == PASSES - 1),
+                )
+
+        def by_slot(bank):
+            return bank[:].rearrange("p (m t) -> p t m", t=PACK)
+
+        def magnitude(n, h):
+            i = n % ROW_TILES
+            mag[n, h] = work.tile([P, PACK, P], F32, name="mag")
+            nc.scalar.activation(out=mag[n, h][:], in_=by_slot(acc[n, h]), func=ACT.Abs, bias=bias[:, i : i + 1])
+
+        def inverse_root(n, h):
+            inv[n, h] = work.tile([P, PACK, P], F32, name="inv%d" % h)
+            nc.scalar.activation(out=inv[n, h][:], in_=mag[n, h][:], func=ACT.Abs_reciprocal_sqrt, bias=0.1)
+
+        def signed_root(n, h):
+            i = n % ROW_TILES
+            pre[n, h] = work.tile([P, PACK, P], F32, name="pre")
+            nc.vector.scalar_tensor_tensor(
+                out=pre[n, h][:],
+                in0=by_slot(acc[n, h]),
+                scalar=bias[:, i : i + 1],
+                in1=inv[n, h][:],
+                op0=ALU.add,
+                op1=ALU.mult,
+            )
+
+        def turn(n, h):
+            turned[n, h] = psum.tile([P, PACK, P], F32, name="turned%d" % h)
+            for t in range(PACK):
+                nc.tensor.transpose(turned[n, h][:, t, :], pre[n, h][:, t, :], ident[:])
+
+        def apply_gain(n, h):
+            if h == 0:
+                z_bf[n] = work.tile([P, HALVES, P, PACK], BF16, name="z_bf", align_bytes=64)
+            nc.vector.tensor_tensor(
+                out=z_bf[n][:, h, :, :],
+                in0=turned[n, h][:].rearrange("p t r -> p r t"),
+                in1=gain[:, h, :].unsqueeze(1).to_broadcast([P, P, PACK]),
+                op=ALU.mult,
+            )
+
+        def quantize_z(n):
+            zq[n] = work.tile([P, HALVES * P], U32, name="zq", align_bytes=64)
+            zs[n] = work.tile([P, HALVES * P], U8, name="zs", align_bytes=64)
+            nc.vector.quantize_mx(
+                out=zq[n][:].bitcast(FP8X4), scales=zs[n][:], in_=z_bf[n][:].rearrange("p h r t -> p (h r t)")
+            )
+
+        def second_product(n):
+            y[n] = psum.tile([P, Q], F32, name="y%d" % (n % ROW_TILES))
+            for h in range(HALVES):
+                nc.tensor.matmul_mx(
+                    out=y[n][:],
+                    lhsT=zq[n][:, h * P : (h + 1) * P].bitcast(FP8X4),
+                    lhsT_scale=zs[n][:, h * P : (h + 1) * P],
+                    rhs=v_w[:, h, :].bitcast(FP4X4),
+                    rhs_scale=v_s[:, h, :],
+                    start=(h == 0),
+                    stop=(h == HALVES - 1),
+                )
+
+        def sum_squares(n):
+            b, i = divmod(n, ROW_TILES)
+            if i == 0:
+                sums[b] = work.tile([P, ROW_TILES], F32, name="sums")
+            squares = work.tile([P, Q], BF16, name="squares")
+            nc.scalar.activation(out=squares[:], in_=y[n][:], func=ACT.Square, accum_out=sums[b][:, i : i + 1])
+
+        def sum_partitions(b):
+            total[b] = psum.tile([P, ROW_TILES], F32, name="total", tag="turned0")
+            nc.tensor.matmul(out=total[b][:], lhsT=ones[:], rhs=sums[b][:], start=True, stop=True)
+
+        def normalizer(b):
+            whole = work.tile([P, 1], F32, name="whole")
+            nc.vector.tensor_reduce(out=whole[:], in_=total[b][:], axis=mybir.AxisListType.X, op=ALU.add)
+            norm[b] = work.tile([P, 1], F32, name="norm")
+            nc.scalar.activation(
+                out=norm[b][:], in_=whole[:], func=ACT.Abs_reciprocal_sqrt, scale=1.0 / (R * Q), bias=1e-5
+            )
+
+        def finish(n, on_scalar):
+            b, i = divmod(n, ROW_TILES)
+            result = results.tile([P, Q], F32, name="result")
+            if on_scalar:
+                nc.scalar.activation(out=result[:], in_=y[n][:], func=ACT.Copy, scale=norm[b][:])
+            else:
+                nc.vector.tensor_scalar(out=result[:], in0=y[n][:], scalar1=norm[b][:], scalar2=None, op0=ALU.mult)
+            nc.sync.dma_start(out=out[b, i * P : (i + 1) * P, :], in_=result[:])
+
+        def unit(n):
+            return 0 <= n < UNITS
+
+        for n in range(-QUANT_LEAD - 1, LAST_STEP + 1):
+            j = n + QUANT_LEAD
+            fill = widen_pieces(j + 1, True)
+            closes = unit(n - 2) and (n - 2) % ROW_TILES == ROW_TILES - 1
+            done = n - ROW_TILES - 1
+            finish_on_scalar = j + 1 < CHUNKS or n + 1 >= UNITS
+            if n == -2:
+                nc.vector.tensor_copy(out=bias[:], in_=c_bf[:, :, 0])
+                nc.vector.tensor_copy(out=gain[:], in_=g_bf[:])
+            if unit(n - 1):
+                apply_gain(n - 1, 0)
+            if closes:
+                sum_partitions((n - 2) // ROW_TILES)
+            if unit(n):
+                signed_root(n, 0)
+            if closes:
+                normalizer((n - 2) // ROW_TILES)
+            if unit(n + 1):
+                first_product(n + 1, 0)
+            if unit(n):
+                turn(n, 0)
+            if unit(n - 1):
+                apply_gain(n - 1, 1)
+            if unit(n):
+                signed_root(n, 1)
+            if unit(n + 1):
+                magnitude(n + 1, 0)
+            if unit(done) and finish_on_scalar:
+                finish(done, True)
+            elif fill:
+                widen(fill.pop(), True)
+            if unit(n + 1):
+                inverse_root(n + 1, 0)
+                first_product(n + 1, 1)
+            if unit(n - 1):
+                quantize_z(n - 1)
+            if unit(done) and not finish_on_scalar:
+                finish(done, False)
+            if unit(n - 1):
+                second_product(n - 1)
+            if unit(n):
+                turn(n, 1)
+            if 0 <= j < CHUNKS:
+                interleave(j)
+            if unit(n + 1):
+                magnitude(n + 1, 1)
+            if unit(n - 1):
+                sum_squares(n - 1)
+            elif fill:
+                widen(fill.pop(), True)
+            if unit(n + 1):
+                inverse_root(n + 1, 1)
+            for piece in fill:
+                widen(piece, True)
+            for piece in widen_pieces(j + 1, False):
+                widen(piece, False)
+            if 0 <= j < CHUNKS:
+                quantize_x(j)
+        for n in range(UNITS - ROW_TILES + 1, UNITS):
+            finish(n, n % 2 == 0)

@@ -26,22 +26,16 @@ HALVES = D // BANK
 ROW_TILES = R // P
 UNITS = B * ROW_TILES
 CHUNKS = B * HALVES * PASSES
-QUANT_LEAD = 5
+QUANT_LEAD = 3
 LAST_STEP = UNITS + 1
+WIDEN_LEAD = 2
+GPSIMD_SHARE = 320
+GPSIMD_FROM = 4
+INTER_BUFS = 1
 
 
-def scalar_share(step):
-    if step == -QUANT_LEAD - 1:
-        return 1024
-    if step < -1:
-        return 1792
-    if step == -1:
-        return 512
-    if step == 0:
-        return 1024
-    if step < 5:
-        return 1536
-    return 1408
+def scalar_share(chunk):
+    return [1024,1536,1536,1536,0,1536,1536,1536,896,896,896,896,896,896,896,896][chunk]
 
 
 def tile_tuckertwopowerpooling_w4_kernel(
@@ -92,10 +86,10 @@ def tile_tuckertwopowerpooling_w4_kernel(
                     in_=scales[:, 4 * q : 4 * q + 4, :].rearrange("k r n -> r k n").bitcast(I32),
                 )
 
-        load_x(0)
         nc.sync.dma_start(
             out=row_scale[:], in_=x_scale.rearrange("o (k p t) e -> p (o k) (t e)", p=P, t=PACK)
         )
+        load_x(0)
         load_x(1)
         load_x(2)
         load_weight(u_w, u_s, u_words, u_scales)
@@ -114,7 +108,7 @@ def tile_tuckertwopowerpooling_w4_kernel(
         def widen_pieces(j, on_scalar):
             if not 0 <= j < CHUNKS:
                 return []
-            share = scalar_share(j - QUANT_LEAD - 1)
+            share = scalar_share(j)
             pieces = []
             for t in range(PACK):
                 cut = min(max(share - t * BANK, 0), BANK)
@@ -126,7 +120,7 @@ def tile_tuckertwopowerpooling_w4_kernel(
         def widen(piece, on_scalar):
             j, t, lo, hi = piece
             if j not in wide:
-                wide[j] = work.tile([P, PACK, BANK], BF16, name="wide", bufs=3)
+                wide[j] = work.tile([P, PACK, BANK], BF16, name="wide", bufs=WIDEN_LEAD + 2)
             src = xb[j][:, t, lo:hi].bitcast(FP8)
             factor = row_scale[:, j % 2, t : t + 1]
             if on_scalar:
@@ -136,12 +130,24 @@ def tile_tuckertwopowerpooling_w4_kernel(
                     out=wide[j][:, t, lo:hi], in0=src, scalar1=factor, scalar2=None, op0=ALU.mult
                 )
 
-        def interleave(j):
-            inter[j] = work.tile([P, BANK, PACK], BF16, name="inter", align_bytes=64)
-            nc.vector.tensor_copy(
-                out=inter[j][:].rearrange("p (c i) t -> p c t i", i=4),
-                in_=wide[j][:].rearrange("p t (c i) -> p c t i", i=4),
-            )
+        def interleave(j, on_gpsimd):
+            share = GPSIMD_SHARE if j >= GPSIMD_FROM else 0
+            if j not in inter:
+                inter[j] = work.tile([P, BANK, PACK], BF16, name="inter", align_bytes=64, bufs=INTER_BUFS)
+            if on_gpsimd and share:
+                nc.gpsimd.tensor_scalar(
+                    out=inter[j][:, :share, :],
+                    in0=wide[j][:, :, :share].rearrange("p t d -> p d t"),
+                    scalar1=1.0,
+                    scalar2=0.0,
+                    op0=ALU.mult,
+                    op1=ALU.add,
+                )
+            if not on_gpsimd and share < BANK:
+                nc.vector.tensor_copy(
+                    out=inter[j][:, share:, :].rearrange("p (c i) t -> p c t i", i=4),
+                    in_=wide[j][:, :, share:].rearrange("p t (c i) -> p c t i", i=4),
+                )
 
         def quantize_x(j):
             xq[j] = codes.tile([P, BANK], U32, name="xq", align_bytes=64)
@@ -150,11 +156,14 @@ def tile_tuckertwopowerpooling_w4_kernel(
                 out=xq[j][:].bitcast(FP8X4), scales=xs[j][:], in_=inter[j][:].rearrange("p d t -> p (d t)")
             )
 
+        def place(n, h):
+            return n // 4, (n // 2) % 2, 2 * (n % 2) + h
+
         def first_product(n, h):
-            b, i = divmod(n, ROW_TILES)
+            b, half, i = place(n, h)
             acc[n, h] = psum.tile([P, BANK], F32, name="acc%d" % h)
             for k in range(PASSES):
-                j = 4 * b + 2 * h + k
+                j = 4 * b + 2 * half + k
                 nc.tensor.matmul_mx(
                     out=acc[n, h][:],
                     lhsT=u_w[:, k, 2 * P * i : 2 * P * (i + 1)].bitcast(FP4X4),
@@ -169,7 +178,7 @@ def tile_tuckertwopowerpooling_w4_kernel(
             return bank[:].rearrange("p (m t) -> p t m", t=PACK)
 
         def magnitude(n, h):
-            i = n % ROW_TILES
+            i = place(n, h)[2]
             mag[n, h] = work.tile([P, PACK, P], F32, name="mag")
             nc.scalar.activation(out=mag[n, h][:], in_=by_slot(acc[n, h]), func=ACT.Abs, bias=bias[:, i : i + 1])
 
@@ -178,7 +187,7 @@ def tile_tuckertwopowerpooling_w4_kernel(
             nc.scalar.activation(out=inv[n, h][:], in_=mag[n, h][:], func=ACT.Abs_reciprocal_sqrt, bias=0.1)
 
         def signed_root(n, h):
-            i = n % ROW_TILES
+            i = place(n, h)[2]
             pre[n, h] = work.tile([P, PACK, P], F32, name="pre")
             nc.vector.scalar_tensor_tensor(
                 out=pre[n, h][:],
@@ -195,123 +204,152 @@ def tile_tuckertwopowerpooling_w4_kernel(
                 nc.tensor.transpose(turned[n, h][:, t, :], pre[n, h][:, t, :], ident[:])
 
         def apply_gain(n, h):
-            if h == 0:
-                z_bf[n] = work.tile([P, HALVES, P, PACK], BF16, name="z_bf", align_bytes=64)
+            half = place(n, h)[1]
+            z_bf[n, h] = work.tile([P, P, PACK], BF16, name="z_bf", align_bytes=64, bufs=3)
             nc.vector.tensor_tensor(
-                out=z_bf[n][:, h, :, :],
+                out=z_bf[n, h][:],
                 in0=turned[n, h][:].rearrange("p t r -> p r t"),
-                in1=gain[:, h, :].unsqueeze(1).to_broadcast([P, P, PACK]),
+                in1=gain[:, half, :].unsqueeze(1).to_broadcast([P, P, PACK]),
                 op=ALU.mult,
             )
 
-        def quantize_z(n):
-            zq[n] = work.tile([P, HALVES * P], U32, name="zq", align_bytes=64)
-            zs[n] = work.tile([P, HALVES * P], U8, name="zs", align_bytes=64)
+        def quantize_z(n, h):
+            key = place(n, h)
+            zq[key] = codes.tile([P, P], U32, name="zq", align_bytes=64)
+            zs[key] = codes.tile([P, P], U8, name="zs", align_bytes=64)
             nc.vector.quantize_mx(
-                out=zq[n][:].bitcast(FP8X4), scales=zs[n][:], in_=z_bf[n][:].rearrange("p h r t -> p (h r t)")
+                out=zq[key][:].bitcast(FP8X4), scales=zs[key][:], in_=z_bf[n, h][:].rearrange("p r t -> p (r t)")
             )
 
-        def second_product(n):
-            y[n] = psum.tile([P, Q], F32, name="y%d" % (n % ROW_TILES))
-            for h in range(HALVES):
-                nc.tensor.matmul_mx(
-                    out=y[n][:],
-                    lhsT=zq[n][:, h * P : (h + 1) * P].bitcast(FP8X4),
-                    lhsT_scale=zs[n][:, h * P : (h + 1) * P],
-                    rhs=v_w[:, h, :].bitcast(FP4X4),
-                    rhs_scale=v_s[:, h, :],
-                    start=(h == 0),
-                    stop=(h == HALVES - 1),
+        def second_product(b, i, half):
+            if half == 0:
+                y[b, i] = psum.tile([P, Q], F32, name="y%d" % i)
+            nc.tensor.matmul_mx(
+                out=y[b, i][:],
+                lhsT=zq[b, half, i][:].bitcast(FP8X4),
+                lhsT_scale=zs[b, half, i][:],
+                rhs=v_w[:, half, :].bitcast(FP4X4),
+                rhs_scale=v_s[:, half, :],
+                start=(half == 0),
+                stop=(half == HALVES - 1),
+            )
+
+        def sum_squares(b, i):
+            sums[b, i] = work.tile([P, 1], F32, name="sums%d" % i)
+            squares = work.tile([P, Q], BF16, name="squares")
+            nc.scalar.activation(out=squares[:], in_=y[b, i][:], func=ACT.Square, accum_out=sums[b, i][:])
+
+        def sum_partitions(b, tiles):
+            for i in tiles:
+                if i == 0:
+                    total[b] = psum.tile([P, 1], F32, name="total", tag="turned1")
+                nc.tensor.matmul(
+                    out=total[b][:], lhsT=ones[:], rhs=sums[b, i][:], start=(i == 0), stop=(i == ROW_TILES - 1)
                 )
 
-        def sum_squares(n):
-            b, i = divmod(n, ROW_TILES)
-            if i == 0:
-                sums[b] = work.tile([P, ROW_TILES], F32, name="sums")
-            squares = work.tile([P, Q], BF16, name="squares")
-            nc.scalar.activation(out=squares[:], in_=y[n][:], func=ACT.Square, accum_out=sums[b][:, i : i + 1])
-
-        def sum_partitions(b):
-            total[b] = psum.tile([P, ROW_TILES], F32, name="total", tag="turned0")
-            nc.tensor.matmul(out=total[b][:], lhsT=ones[:], rhs=sums[b][:], start=True, stop=True)
-
         def normalizer(b):
-            whole = work.tile([P, 1], F32, name="whole")
-            nc.vector.tensor_reduce(out=whole[:], in_=total[b][:], axis=mybir.AxisListType.X, op=ALU.add)
             norm[b] = work.tile([P, 1], F32, name="norm")
             nc.scalar.activation(
-                out=norm[b][:], in_=whole[:], func=ACT.Abs_reciprocal_sqrt, scale=1.0 / (R * Q), bias=1e-5
+                out=norm[b][:], in_=total[b][:], func=ACT.Abs_reciprocal_sqrt, scale=1.0 / (R * Q), bias=1e-5
             )
 
-        def finish(n, on_scalar):
-            b, i = divmod(n, ROW_TILES)
+        def finish(b, i, on_scalar):
             result = results.tile([P, Q], F32, name="result")
             if on_scalar:
-                nc.scalar.activation(out=result[:], in_=y[n][:], func=ACT.Copy, scale=norm[b][:])
+                nc.scalar.activation(out=result[:], in_=y[b, i][:], func=ACT.Copy, scale=norm[b][:])
             else:
-                nc.vector.tensor_scalar(out=result[:], in0=y[n][:], scalar1=norm[b][:], scalar2=None, op0=ALU.mult)
+                nc.vector.tensor_scalar(out=result[:], in0=y[b, i][:], scalar1=norm[b][:], scalar2=None, op0=ALU.mult)
             nc.sync.dma_start(out=out[b, i * P : (i + 1) * P, :], in_=result[:])
 
         def unit(n):
             return 0 <= n < UNITS
 
-        for n in range(-QUANT_LEAD - 1, LAST_STEP + 1):
+        for n in range(-QUANT_LEAD - WIDEN_LEAD, LAST_STEP):
             j = n + QUANT_LEAD
-            fill = widen_pieces(j + 1, True)
-            closes = unit(n - 2) and (n - 2) % ROW_TILES == ROW_TILES - 1
-            done = n - ROW_TILES - 1
-            finish_on_scalar = j + 1 < CHUNKS or n + 1 >= UNITS
+            fill = widen_pieces(j + WIDEN_LEAD, True)
+            closes = unit(n - 2) and (n - 2) % 4 == 3
+            second = unit(n - 1) and place(n - 1, 0)[1] == 1
+            sample, tile0, tile1 = (n - 1) // 4, place(n - 1, 0)[2], place(n - 1, 1)[2]
+            widening = j < CHUNKS
+            done = []
+            late = n if widening else n - 1
+            if late >= 5 and late % 4 in (1, 2):
+                done = [((late - 5) // 4, 2 * ((late - 1) % 4) + h) for h in range(2)]
             if n == -2:
                 nc.vector.tensor_copy(out=bias[:], in_=c_bf[:, :, 0])
                 nc.vector.tensor_copy(out=gain[:], in_=g_bf[:])
+            if 0 <= j < CHUNKS:
+                interleave(j, True)
             if unit(n - 1):
                 apply_gain(n - 1, 0)
-            if closes:
-                sum_partitions((n - 2) // ROW_TILES)
             if unit(n):
                 signed_root(n, 0)
-            if closes:
-                normalizer((n - 2) // ROW_TILES)
             if unit(n + 1):
                 first_product(n + 1, 0)
             if unit(n):
                 turn(n, 0)
+            if n == UNITS:
+                quantize_z(n - 1, 0)
             if unit(n - 1):
                 apply_gain(n - 1, 1)
             if unit(n):
                 signed_root(n, 1)
             if unit(n + 1):
                 magnitude(n + 1, 0)
-            if unit(done) and finish_on_scalar:
-                finish(done, True)
-            elif fill:
+            if fill:
                 widen(fill.pop(), True)
             if unit(n + 1):
                 inverse_root(n + 1, 0)
                 first_product(n + 1, 1)
+            if closes:
+                sum_partitions((n - 2) // 4, range(ROW_TILES))
+            if done and second:
+                finish(done[0][0], done[0][1], True)
+                finish(done[1][0], done[1][1], True)
+                done = []
+            if second:
+                second_product(sample, tile0, 0)
+                second_product(sample, tile1, 0)
             if unit(n - 1):
-                quantize_z(n - 1)
-            if unit(done) and not finish_on_scalar:
-                finish(done, False)
-            if unit(n - 1):
-                second_product(n - 1)
-            if unit(n):
+                if n < UNITS:
+                    quantize_z(n - 1, 0)
+                if second:
+                    second_product(sample, tile0, 1)
+                quantize_z(n - 1, 1)
+                if second:
+                    second_product(sample, tile1, 1)
+            if unit(n) and not closes:
                 turn(n, 1)
-            if 0 <= j < CHUNKS:
-                interleave(j)
             if unit(n + 1):
                 magnitude(n + 1, 1)
-            if unit(n - 1):
-                sum_squares(n - 1)
+            if closes:
+                normalizer((n - 2) // 4)
+                turn(n, 1)
+            if second:
+                sum_squares(sample, tile0)
+            elif done and widening:
+                finish(done[0][0], done[0][1], True)
             elif fill:
                 widen(fill.pop(), True)
             if unit(n + 1):
                 inverse_root(n + 1, 1)
+            if done and not widening:
+                finish(done[0][0], done[0][1], False)
+            if n == UNITS:
+                sum_partitions(sample, range(ROW_TILES - 1))
+            if second:
+                sum_squares(sample, tile1)
+            elif done:
+                finish(done[1][0], done[1][1], widening or True)
             for piece in fill:
                 widen(piece, True)
-            for piece in widen_pieces(j + 1, False):
+            if 0 <= j < CHUNKS:
+                interleave(j, False)
+            for piece in widen_pieces(j + WIDEN_LEAD, False):
                 widen(piece, False)
             if 0 <= j < CHUNKS:
                 quantize_x(j)
-        for n in range(UNITS - ROW_TILES + 1, UNITS):
-            finish(n, n % 2 == 0)
+        sum_partitions(B - 1, [ROW_TILES - 1])
+        normalizer(B - 1)
+        for i in range(ROW_TILES):
+            finish(B - 1, i, i % 2 == 0)

from contextlib import ExitStack

import concourse.mybir as mybir
from concourse.masks import make_identity

B, S, D, R, Q = 4, 1024, 1024, 512, 512
FLOPS = B * (2 * S * R * D + 2 * R * D * Q)

F32 = mybir.dt.float32
BF16 = mybir.dt.bfloat16
I32 = mybir.dt.int32
U32 = mybir.dt.uint32
U8 = mybir.dt.uint8
FP8 = mybir.dt.float8_e4m3fn
FP8X4 = mybir.dt.float8_e4m3fn_x4
FP4X4 = mybir.dt.float4_e2m1fn_x4
ACT = mybir.ActivationFunctionType
ALU = mybir.AluOpType

P = 128
PACK = 4
K_PASS = P * PACK
BANK = 512
PASSES = S // K_PASS
HALVES = D // BANK
ROW_TILES = R // P
UNITS = B * ROW_TILES
CHUNKS = B * HALVES * PASSES
QUANT_LEAD = 3
LAST_STEP = UNITS + 1
WIDEN_LEAD = 2
GPSIMD_SHARE = 320
GPSIMD_FROM = 4
INTER_BUFS = 1


def scalar_share(chunk):
    return [1024,1536,1536,1536,0,1536,1536,1536,896,896,896,896,896,896,896,896][chunk]


def tile_tuckertwopowerpooling_w4_kernel(
    tc, x_bytes, x_scale, u_words, u_scales, c, g, v_words, v_scales, out
):
    nc = tc.nc
    with ExitStack() as ctx:
        keep = ctx.enter_context(tc.tile_pool(name="keep", bufs=1))
        work = ctx.enter_context(tc.tile_pool(name="work", bufs=2))
        codes = ctx.enter_context(tc.tile_pool(name="codes", bufs=2 * HALVES * PASSES))
        results = ctx.enter_context(tc.tile_pool(name="results", bufs=4))
        psum = ctx.enter_context(tc.psum_pool(name="psum", bufs=1))
        ctx.enter_context(tc.manual_schedule())
        ctx.enter_context(nc.allow_non_contiguous_dma(reason="small vectors go one row to a partition"))

        u_w = keep.tile([P, PASSES, 2 * R], U8, name="u_w", align_bytes=64)
        u_s = keep.tile([P, PASSES, R], U8, name="u_s", align_bytes=64)
        v_w = keep.tile([P, HALVES, 2 * Q], U8, name="v_w", align_bytes=64)
        v_s = keep.tile([P, HALVES, Q], U8, name="v_s", align_bytes=64)
        row_scale = keep.tile([P, PASSES, PACK], F32, name="row_scale")
        c_bf = keep.tile([P, ROW_TILES, 2], BF16, name="c_bf")
        g_bf = keep.tile([P, HALVES, PACK], BF16, name="g_bf")
        bias = keep.tile([P, ROW_TILES], F32, name="bias")
        gain = keep.tile([P, HALVES, PACK], F32, name="gain")
        ident = keep.tile([P, P], F32, name="ident")
        ones = keep.tile([P, P], F32, name="ones")

        nc.vector.memset(u_s[:].rearrange("p g n -> p (g n)").bitcast(I32), 0)
        nc.vector.memset(v_s[:].rearrange("p g n -> p (g n)").bitcast(I32), 0)
        make_identity(nc, ident[:])
        nc.gpsimd.memset(ones[:], 1.0)

        xb = {}

        def load_x(j):
            b, h, k = j // 4, (j // 2) % 2, j % 2
            xb[j] = keep.tile([P, PACK, BANK], U8, name="xb%d" % j)
            rows = x_bytes[b, k * K_PASS : (k + 1) * K_PASS, h * BANK : (h + 1) * BANK]
            nc.sync.dma_start(out=xb[j][:], in_=rows.rearrange("(p t) d -> p t d", t=PACK))

        def load_weight(words_sb, scales_sb, words, scales):
            nc.sync.dma_start(
                out=words_sb[:].bitcast(I32), in_=words.rearrange("k p n -> p k n").bitcast(I32)
            )
            for q in range(4):
                nc.sync.dma_start(
                    out=scales_sb[32 * q : 32 * q + 4, :, :].bitcast(I32),
                    in_=scales[:, 4 * q : 4 * q + 4, :].rearrange("k r n -> r k n").bitcast(I32),
                )

        nc.sync.dma_start(
            out=row_scale[:], in_=x_scale.rearrange("o (k p t) e -> p (o k) (t e)", p=P, t=PACK)
        )
        load_x(0)
        load_x(1)
        load_x(2)
        load_weight(u_w, u_s, u_words, u_scales)
        load_x(3)
        nc.sync.dma_start(out=c_bf[:, :, 0:1], in_=c.rearrange("(i p e) -> p i e", p=P, e=1))
        nc.sync.dma_start(out=g_bf[:], in_=g.rearrange("(h p t) -> p h t", p=P, t=PACK))
        load_x(4)
        load_weight(v_w, v_s, v_words, v_scales)
        for j in range(5, CHUNKS):
            load_x(j)

        wide, inter, xq, xs = {}, {}, {}, {}
        acc, mag, inv, pre, turned, z_bf, zq, zs, y = {}, {}, {}, {}, {}, {}, {}, {}, {}
        sums, total, norm = {}, {}, {}

        def widen_pieces(j, on_scalar):
            if not 0 <= j < CHUNKS:
                return []
            share = scalar_share(j)
            pieces = []
            for t in range(PACK):
                cut = min(max(share - t * BANK, 0), BANK)
                lo, hi = (0, cut) if on_scalar else (cut, BANK)
                if hi > lo:
                    pieces.append((j, t, lo, hi))
            return pieces

        def widen(piece, on_scalar):
            j, t, lo, hi = piece
            if j not in wide:
                wide[j] = work.tile([P, PACK, BANK], BF16, name="wide", bufs=WIDEN_LEAD + 2)
            src = xb[j][:, t, lo:hi].bitcast(FP8)
            factor = row_scale[:, j % 2, t : t + 1]
            if on_scalar:
                nc.scalar.activation(out=wide[j][:, t, lo:hi], in_=src, func=ACT.Copy, scale=factor)
            else:
                nc.vector.tensor_scalar(
                    out=wide[j][:, t, lo:hi], in0=src, scalar1=factor, scalar2=None, op0=ALU.mult
                )

        def interleave(j, on_gpsimd):
            share = GPSIMD_SHARE if j >= GPSIMD_FROM else 0
            if j not in inter:
                inter[j] = work.tile([P, BANK, PACK], BF16, name="inter", align_bytes=64, bufs=INTER_BUFS)
            if on_gpsimd and share:
                nc.gpsimd.tensor_scalar(
                    out=inter[j][:, :share, :],
                    in0=wide[j][:, :, :share].rearrange("p t d -> p d t"),
                    scalar1=1.0,
                    scalar2=0.0,
                    op0=ALU.mult,
                    op1=ALU.add,
                )
            if not on_gpsimd and share < BANK:
                nc.vector.tensor_copy(
                    out=inter[j][:, share:, :].rearrange("p (c i) t -> p c t i", i=4),
                    in_=wide[j][:, :, share:].rearrange("p t (c i) -> p c t i", i=4),
                )

        def quantize_x(j):
            xq[j] = codes.tile([P, BANK], U32, name="xq", align_bytes=64)
            xs[j] = codes.tile([P, BANK], U8, name="xs", align_bytes=64)
            nc.vector.quantize_mx(
                out=xq[j][:].bitcast(FP8X4), scales=xs[j][:], in_=inter[j][:].rearrange("p d t -> p (d t)")
            )

        def place(n, h):
            return n // 4, (n // 2) % 2, 2 * (n % 2) + h

        def first_product(n, h):
            b, half, i = place(n, h)
            acc[n, h] = psum.tile([P, BANK], F32, name="acc%d" % h)
            for k in range(PASSES):
                j = 4 * b + 2 * half + k
                nc.tensor.matmul_mx(
                    out=acc[n, h][:],
                    lhsT=u_w[:, k, 2 * P * i : 2 * P * (i + 1)].bitcast(FP4X4),
                    lhsT_scale=u_s[:, k, P * i : P * (i + 1)],
                    rhs=xq[j][:].bitcast(FP8X4),
                    rhs_scale=xs[j][:],
                    start=(k == 0),
                    stop=(k == PASSES - 1),
                )

        def by_slot(bank):
            return bank[:].rearrange("p (m t) -> p t m", t=PACK)

        def magnitude(n, h):
            i = place(n, h)[2]
            mag[n, h] = work.tile([P, PACK, P], F32, name="mag")
            nc.scalar.activation(out=mag[n, h][:], in_=by_slot(acc[n, h]), func=ACT.Abs, bias=bias[:, i : i + 1])

        def inverse_root(n, h):
            inv[n, h] = work.tile([P, PACK, P], F32, name="inv%d" % h)
            nc.scalar.activation(out=inv[n, h][:], in_=mag[n, h][:], func=ACT.Abs_reciprocal_sqrt, bias=0.1)

        def signed_root(n, h):
            i = place(n, h)[2]
            pre[n, h] = work.tile([P, PACK, P], F32, name="pre")
            nc.vector.scalar_tensor_tensor(
                out=pre[n, h][:],
                in0=by_slot(acc[n, h]),
                scalar=bias[:, i : i + 1],
                in1=inv[n, h][:],
                op0=ALU.add,
                op1=ALU.mult,
            )

        def turn(n, h):
            turned[n, h] = psum.tile([P, PACK, P], F32, name="turned%d" % h)
            for t in range(PACK):
                nc.tensor.transpose(turned[n, h][:, t, :], pre[n, h][:, t, :], ident[:])

        def apply_gain(n, h):
            half = place(n, h)[1]
            z_bf[n, h] = work.tile([P, P, PACK], BF16, name="z_bf", align_bytes=64, bufs=3)
            nc.vector.tensor_tensor(
                out=z_bf[n, h][:],
                in0=turned[n, h][:].rearrange("p t r -> p r t"),
                in1=gain[:, half, :].unsqueeze(1).to_broadcast([P, P, PACK]),
                op=ALU.mult,
            )

        def quantize_z(n, h):
            key = place(n, h)
            zq[key] = codes.tile([P, P], U32, name="zq", align_bytes=64)
            zs[key] = codes.tile([P, P], U8, name="zs", align_bytes=64)
            nc.vector.quantize_mx(
                out=zq[key][:].bitcast(FP8X4), scales=zs[key][:], in_=z_bf[n, h][:].rearrange("p r t -> p (r t)")
            )

        def second_product(b, i, half):
            if half == 0:
                y[b, i] = psum.tile([P, Q], F32, name="y%d" % i)
            nc.tensor.matmul_mx(
                out=y[b, i][:],
                lhsT=zq[b, half, i][:].bitcast(FP8X4),
                lhsT_scale=zs[b, half, i][:],
                rhs=v_w[:, half, :].bitcast(FP4X4),
                rhs_scale=v_s[:, half, :],
                start=(half == 0),
                stop=(half == HALVES - 1),
            )

        def sum_squares(b, i):
            sums[b, i] = work.tile([P, 1], F32, name="sums%d" % i)
            squares = work.tile([P, Q], BF16, name="squares")
            nc.scalar.activation(out=squares[:], in_=y[b, i][:], func=ACT.Square, accum_out=sums[b, i][:])

        def sum_partitions(b, tiles):
            for i in tiles:
                if i == 0:
                    total[b] = psum.tile([P, 1], F32, name="total", tag="turned1")
                nc.tensor.matmul(
                    out=total[b][:], lhsT=ones[:], rhs=sums[b, i][:], start=(i == 0), stop=(i == ROW_TILES - 1)
                )

        def normalizer(b):
            norm[b] = work.tile([P, 1], F32, name="norm")
            nc.scalar.activation(
                out=norm[b][:], in_=total[b][:], func=ACT.Abs_reciprocal_sqrt, scale=1.0 / (R * Q), bias=1e-5
            )

        def finish(b, i, on_scalar):
            result = results.tile([P, Q], F32, name="result")
            if on_scalar:
                nc.scalar.activation(out=result[:], in_=y[b, i][:], func=ACT.Copy, scale=norm[b][:])
            else:
                nc.vector.tensor_scalar(out=result[:], in0=y[b, i][:], scalar1=norm[b][:], scalar2=None, op0=ALU.mult)
            nc.sync.dma_start(out=out[b, i * P : (i + 1) * P, :], in_=result[:])

        def unit(n):
            return 0 <= n < UNITS

        for n in range(-QUANT_LEAD - WIDEN_LEAD, LAST_STEP):
            j = n + QUANT_LEAD
            fill = widen_pieces(j + WIDEN_LEAD, True)
            closes = unit(n - 2) and (n - 2) % 4 == 3
            second = unit(n - 1) and place(n - 1, 0)[1] == 1
            sample, tile0, tile1 = (n - 1) // 4, place(n - 1, 0)[2], place(n - 1, 1)[2]
            widening = j < CHUNKS
            done = []
            late = n if widening else n - 1
            if late >= 5 and late % 4 in (1, 2):
                done = [((late - 5) // 4, 2 * ((late - 1) % 4) + h) for h in range(2)]
            if n == -2:
                nc.vector.tensor_copy(out=bias[:], in_=c_bf[:, :, 0])
                nc.vector.tensor_copy(out=gain[:], in_=g_bf[:])
            if 0 <= j < CHUNKS:
                interleave(j, True)
            if unit(n - 1):
                apply_gain(n - 1, 0)
            if unit(n):
                signed_root(n, 0)
            if unit(n + 1):
                first_product(n + 1, 0)
            if unit(n):
                turn(n, 0)
            if n == UNITS:
                quantize_z(n - 1, 0)
            if unit(n - 1):
                apply_gain(n - 1, 1)
            if unit(n):
                signed_root(n, 1)
            if unit(n + 1):
                magnitude(n + 1, 0)
            if fill:
                widen(fill.pop(), True)
            if unit(n + 1):
                inverse_root(n + 1, 0)
                first_product(n + 1, 1)
            if closes:
                sum_partitions((n - 2) // 4, range(ROW_TILES))
            if done and second:
                finish(done[0][0], done[0][1], True)
                finish(done[1][0], done[1][1], True)
                done = []
            if second:
                second_product(sample, tile0, 0)
                second_product(sample, tile1, 0)
            if unit(n - 1):
                if n < UNITS:
                    quantize_z(n - 1, 0)
                if second:
                    second_product(sample, tile0, 1)
                quantize_z(n - 1, 1)
                if second:
                    second_product(sample, tile1, 1)
            if unit(n) and not closes:
                turn(n, 1)
            if unit(n + 1):
                magnitude(n + 1, 1)
            if closes:
                normalizer((n - 2) // 4)
                turn(n, 1)
            if second:
                sum_squares(sample, tile0)
            elif done and widening:
                finish(done[0][0], done[0][1], True)
            elif fill:
                widen(fill.pop(), True)
            if unit(n + 1):
                inverse_root(n + 1, 1)
            if done and not widening:
                finish(done[0][0], done[0][1], False)
            if n == UNITS:
                sum_partitions(sample, range(ROW_TILES - 1))
            if second:
                sum_squares(sample, tile1)
            elif done:
                finish(done[1][0], done[1][1], widening or True)
            for piece in fill:
                widen(piece, True)
            if 0 <= j < CHUNKS:
                interleave(j, False)
            for piece in widen_pieces(j + WIDEN_LEAD, False):
                widen(piece, False)
            if 0 <= j < CHUNKS:
                quantize_x(j)
        sum_partitions(B - 1, [ROW_TILES - 1])
        normalizer(B - 1)
        for i in range(ROW_TILES):
            finish(B - 1, i, i % 2 == 0)
